import numpy as np, ml_dtypes
CORES = [1,5,17,21,33,37,49,53]
N = 8
BF = ml_dtypes.bfloat16
E, D, R, NB, M, PH, P = 4096, 512, 512, 2, 8, 3, 3
S = NB + 2 - PH % 2
def link(rng, a, b):
    k = np.arange(E); k[:D] += D; k[a] = b
    s = np.setdiff1d(np.arange(D, E), a); t = np.setdiff1d(np.concatenate([np.arange(D), np.arange(2 * D, E)]), b)
    k[s] = rng.permutation(t)
    return k
def near(rng, n):
    return link(rng, 2 * D + rng.permutation(R)[:n], rng.permutation(D)[:n])
def ways(rng, late, fresh):
    pool = 2 * D + R + rng.permutation(E - 2 * D - R); at = [0]; o = 2 * D + rng.permutation(R); tab = [([], []), ([], [])]
    def join(a, b, t):
        tab[t & 1][0].append(a); tab[t & 1][1].append(b)
    def go(a, t, n):
        for i in range(t, t + n):
            b = pool[at[0]:at[0] + len(a)]; at[0] += len(a)
            join(a, b, i); a = b
        return a
    if late:
        join(go(o[:D], 0, PH), rng.permutation(D), PH); go(o[D:], 0, PH + 1)
    else:
        w = go(o[:D], 0, PH - 1); join(w, rng.permutation(D), PH - 1)
        u = go(o[D:], 0, 2 * PH); s = go(D + np.arange(D), PH, PH)
        m = np.concatenate([u, s]); to = m
        if PH % 2 == 0:
            m = np.concatenate([m, w]); to = np.concatenate([to, o[:D]])
        if fresh: go(m, 2 * PH, 1)
        else: join(m, rng.permutation(to), 2 * PH)
    return [link(rng, np.concatenate(a), np.concatenate(b)) for a, b in tab]
def both(rng, one):
    p = [[one(r, g) for g in range(8)] for r in range(N)]
    return [np.array([[p[r][g][i] for g in range(8)] for r in range(N)]) for i in range(2)]
def some(rng):
    return both(rng, lambda r, g: (near(rng, int(rng.integers(D // 8, D // 2))), near(rng, int(rng.integers(0, D // 2)))))
def values(rng):
    e = rng.choice(np.array([0.5, 1.0, 2.0]), (N, 8, 1, E))
    x = np.minimum(np.floor(16 * rng.random((N, 8, 16, E)) ** e), 15).astype(np.int64)
    q = np.minimum(np.floor(16 * rng.random((N, 8, 16, R)) * rng.random((N, 8, 1, R))), 15).astype(np.int64)
    return x, q
def pack(k, x, q):
    return {"k0": k[0].astype(np.int32), "k1": k[1].astype(np.int32), "x": np.ascontiguousarray(x.reshape(N, 128, E)).astype(np.float32).astype(BF),
            "q": np.ascontiguousarray(q.reshape(N, 128, R)).astype(np.float32).astype(BF)}
def setup_inputs(rng):
    x, q = values(rng)
    return pack(some(rng), x, q)
def setup_inputs_full(rng):
    x, q = values(rng)
    def one(r, g):
        if r < S: return ways(rng, False, r > NB)
        if g == 6: return ways(rng, True, False)
        if g == 7: return [link(rng, D + rng.permutation(D), rng.permutation(D)) for i in range(2)]
        n = (D, D, D - 1, D, 1, D // 2)[g]
        return near(rng, n), near(rng, D // 4)
    q[:, :5] = 0
    x[:S] = rng.integers(13, 16, (S, 8, 16, E)); q[:S] = rng.integers(0, 14, (S, 8, 16, R))
    x[S:, 6] = rng.integers(13, 16, (N - S, 16, E)); q[S:, 6] = rng.integers(0, 14, (N - S, 16, R))
    return pack(both(rng, one), x, q)
def setup_inputs_ties(rng):
    hi = rng.integers(4, 16, (N, 8, 1, 1)); cnt = rng.integers(M - 1, M + 2, (N, 8, 1, E)); off = 2 * rng.integers(0, 2, (N, 8, 1, E))
    top = np.argsort(rng.random((N, 8, E, 16)), axis=-1).transpose(0, 1, 3, 2) < cnt
    x = hi - 1 + top - off; q = np.broadcast_to(hi - 2 * rng.integers(0, 2, (N, 8, 1, R)), (N, 8, 16, R))
    return pack(some(rng), x, q)
def setup_inputs_chain(rng):
    def one(r, g):
        h = D // 2
        return [link(rng, np.concatenate([2 * D + rng.permutation(R)[:h], D + rng.permutation(D)[:D - h]]), rng.permutation(D)) for i in range(2)]
    x = rng.integers(10, 16, (N, 8, 16, E)); q = rng.integers(0, 9, (N, 8, 16, R))
    return pack(both(rng, one), x, q)
def setup_inputs_ends(rng):
    x, q = values(rng)
    def one(r, g):
        a = np.arange(2 * D, E)
        if g == 2: return [link(rng, a, a) for i in range(2)]
        if g == 3:
            k = near(rng, D // 2); return k, k
        u = np.array([2 * D, 2 * D + R - 1, 2 * D + 1]); w = np.array([0, D - 1, E - 1])
        return link(rng, u, w), link(rng, u, w[::-1])
    x[:, 0] = 0; q[:, 0] = 0; x[:, 1] = 15; q[:, 1] = 15; x[:, 6] = 0; q[:, 6] = rng.integers(0, 3, (N, 1, R))
    q[..., 0] = 0; q[..., 1] = 0; q[..., R - 1] = 0
    return pack(both(rng, one), x, q)
def setup_inputs_spread(rng):
    x = np.minimum(np.floor(np.exp2(4 * rng.random((N, 8, 1, E))) * rng.random((N, 8, 16, E))), 15).astype(np.int64)
    q = np.minimum(np.floor(np.exp2(4 * rng.random((N, 8, 1, R))) * rng.random((N, 8, 16, R))), 15).astype(np.int64)
    c = np.array([0, 1, D // 2, D])
    return pack(both(rng, lambda r, g: (near(rng, int(rng.choice(c))), near(rng, int(rng.choice(c))))), x, q)
def check_inputs(d):
    bad = []
    for k in ("k0", "k1"):
        v = np.asarray(d[k]).astype(np.int64)
        if np.any(np.sort(v, axis=-1) != np.arange(E)): bad.append(k + " is no permutation")
        if np.any(v[..., :D] != D + np.arange(D)): bad.append("doors of " + k)
    for k in ("x", "q"):
        v = np.asarray(d[k]).astype(np.float64)
        if not np.all((v >= 0) & (v <= 15) & (v == np.rint(v))): bad.append("range of " + k)
    return bad
def reference(k0, k1, x, q):
    k = np.stack([k0, k1]).astype(np.int64)
    X = x.astype(np.float32).astype(np.int64).reshape(N, 8, 16, E)
    Q = np.concatenate([q.astype(np.float32).astype(np.int64).reshape(N, 8, 16, R), np.zeros((N, 8, 16, D), np.int64)], axis=3)
    first = np.concatenate([2 * D + np.arange(R), D + np.arange(D)])
    v = np.tile(first, (N, 8, 1)); b = v.copy()
    act = np.zeros((N, 8, R + D), bool); act[:, :, :R] = True
    mark = np.zeros((N, 8, E), bool); mark[:, :, 2 * D:2 * D + R] = True
    turn = np.zeros((N, 8, E), np.int64); wait = np.zeros((N, 8, R + D), bool)
    def enough(hi, lo, axis):
        return np.add.reduce((hi >= lo).astype(np.int64), axis=axis) >= M
    def retreat(m):
        Q[:] = Q - m[:, :, None, :].astype(np.int64)
        n, g, w = np.nonzero(m & (b != v))
        p = b[n, g, w]; o = v[n, g, w]; h = turn[n, g, p]; back = k[h, n, g, p]
        xo = X[n, g, :, o]; xp = X[n, g, :, p]
        k[h, n, g, p] = np.where(enough(xo, xp, 1), o, p)
        X[n, g, :, p] = np.maximum(xp, xo - 1)
        b[n, g, w] = back; v[n, g, w] = p
    for t in range(PH * P):
        f = t & 1
        go = act & (v >= D)
        c = np.take_along_axis(k[f], v, 2)
        ok = go & ~np.take_along_axis(mark, c, 2) & enough(np.take_along_axis(X, c[:, :, None, :], 3), Q, 2)
        n, g, w = np.nonzero(ok); o = v[n, g, w]; to = c[n, g, w]
        k[f, n, g, o] = b[n, g, w]; turn[n, g, o] = f; mark[n, g, to] = True
        Q[n, g, :, w] = np.maximum(Q[n, g, :, w], X[n, g, :, to]) - 2
        b[n, g, w] = o; v[n, g, w] = to
        retreat(go & ~ok)
        if t % PH == PH - 1:
            on = act & (v < D); stay = on & wait; new = on & ~wait
            n, g, w = np.nonzero(new); j = v[n, g, w]; to = (n + 1 + j // (D // NB)) % N
            Q[to, g, :, R + j] = Q[n, g, :, w]; act[to, g, R + j] = True; mark[to, g, D + j] = True
            n, g, w = np.nonzero(stay); j = v[n, g, w]; to = (n + 1 + j // (D // NB)) % N
            X[n, g, :, j] = X[to, g, :, D + j]
            retreat(stay)
            wait = new
    return {"yk0": k[0].astype(np.float32), "yk1": k[1].astype(np.float32), "yx": X.reshape(N, 128, E).astype(np.float32).astype(BF)}

from concourse.bass import DstId, RemoteDMATransfer
from concourse.mybir import AluOpType as AL, ActivationFunctionType as AF

F, B, I, U = "float32", "bfloat16", "int32", "uint16"
SL, DUM, RV2 = 4096, 12288, 13312
NW = 24
_SB = {
    "KI": (512, I), "KL": (512, I), "KH": (512, I), "DL": (512, B), "DH": (512, B), "KF": (512, F),
    "TB": (5120, B), "WX": (13824, B), "Q": (1024, B), "TQ": (1040, B), "RQ": (512, B), "QG": (1024, B), "GV": (1024, B),
    "KG": (1024, B), "CMP": (1024, B), "CM2": (3072, B), "BASE": (1024, B), "TT": (2048, B), "T1": (2048, B), "T2": (1024, B),
    "T3": (1024, B), "G8": (1024, B), "WK": (9216, F), "XO": (4096, B), "YK": (4096, F), "KD0": (576, F), "KD1": (576, F),
    "N144": (144, F), "PI": (8, I), "COL": (48, F), "M16": (16, F), "BC": (16, F), "MG": (128, F),
    "A1": (144, B), "A8": (144, B), "AK0": (144, B), "AK1": (144, B), "AX": (144, B), "AKW": (144, B),
    "BO": (128, B), "SB": (2048, B), "I1": (128, B), "IN": (128, B), "I64": (128, B), "I4K": (128, B), "I24": (128, B),
    "F1": (128, F), "FN": (128, F), "XS": (512, F), "UQ": (1024, B),
    "E": (256, F), "J8": (64, F), "KR": (128, F), "KDR": (128, F), "KAD": (64, F), "KDH": (256, F),
    "C": (576, F), "CR": (576, F), "C8": (576, F), "ALT": (576, F), "DC": (512, F), "W": (64 * NW, F), "WI": (128, I),
    "OK": (640, B), "DR": (576, B), "SG": (576, B), "AA": (640, B), "AN": (576, B), "GO": (640, B), "DM": (640, B),
    "RR": (640, B), "ZP": (640, B), "ZZ": (64, B), "WT": (576, B), "H": (576, B), "M": (896, B), "FL": (3072, B),
    "AF": (640, B), "E1": (576, F), "E2": (576, F), "Y": (640, F), "MX": (256, F), "MK": (256, F), "DO": (32, F),
    "c16": (128, U), "s16": (128, U), "o16": (512, U), "x16": (256, U), "k16": (256, U),
}
SCRATCH = {n: ("sbuf", [128, w], d) for n, (w, d) in _SB.items()}
_PS = ["PS%d" % i for i in range(8)]
SCRATCH.update({n: ("psum", [128, 512], F) for n in _PS})
SEMAPHORES = ["sv", "ss", "sp", "sg", "ls", "e0", "e1", "v1", "v2"] + ["d%d" % i for i in range(30)]
CFG = {"cmp": "ss", "xq": "svsv", "kq": "svsv", "uq": "vs", "kg": "vs", "split": (3, 6), "qs": "vv", "ps": "vvvvvvv",
       "tail": "s", "rg": "sv", "lp": "vs", "lc": "sv", "pri": 8.0, "mp": (1.0, 0.0),
       "cyc": 1.04e-3, "pe": 0.5e-3, "ga": 1.5, "sc": 3.8, "fix": 0.05, "lat": 0.1, "dma": 2.0, "rem": 4.0}


def masks(topo, src, a, b):
    ea, eb = topo.engines(src, a), topo.engines(src, b)
    oa, ob = [e for e in ea if e not in eb], [e for e in eb if e not in ea]
    if oa:
        ea = oa
    elif ob:
        eb = ob
    else:
        ea, eb = ea[:len(ea) // 2], eb[len(eb) // 2:]
    return ea, eb


def layout(ops):
    n, lat = len(ops), CFG["lat"]
    users = {}
    for k, o in enumerate(ops):
        for x in o["tiles"]:
            users.setdefault(x, []).append(k)
    pre = [set(o["pre"]) for o in ops]
    soft = [set() for o in ops]
    for x, us in users.items():
        for u in us[1:]:
            soft[us[0]] |= pre[u] - set(us)
    suc = [[] for o in ops]
    for k in range(n):
        for p in pre[k] | soft[k]:
            suc[p].append(k)
    left = [len(pre[k] | soft[k]) for k in range(n)]
    topo_, todo = [], [k for k in range(n) if not left[k]]
    while todo:
        k = todo.pop()
        topo_.append(k)
        for s in suc[k]:
            left[s] -= 1
            if not left[s]:
                todo.append(s)
    bl = [0.0] * n
    for k in reversed(topo_):
        bl[k] = ops[k]["c"] + ops[k]["after"] + lat + max([bl[s] for s in suc[k]] + [0.0]) + ops[k].get("pri", 0.0)
    start, busy, held, bank = [None] * n, {}, {}, {}

    def gap(k, t, extra=()):
        for p in pre[k]:
            t = max(t, start[p] + ops[p]["c"] + ops[p]["after"] + lat)
        for a, b in sorted(busy.setdefault(ops[k]["q"], []) + list(extra)):
            if a >= t + ops[k]["c"]:
                break
            t = max(t, b)
        return t

    for k in sorted(range(n), key=lambda k: ops[k]["c"] - bl[k]):
        if start[k] is not None:
            continue
        if not ops[k]["tiles"]:
            start[k] = gap(k, 0.0)
            busy[ops[k]["q"]].append((start[k], start[k] + ops[k]["c"]))
            continue
        x = ops[k]["tiles"][0]
        best = None
        for b in _PS:
            t = 0.0
            while True:
                put = []
                for u in users[x]:
                    start[u] = gap(u, t, [(s, s + ops[v]["c"]) for v, s in put if ops[v]["q"] == ops[u]["q"]])
                    put.append((u, start[u]))
                a, e = put[0][1], max(s + ops[v]["c"] for v, s in put) + lat
                hit = [y for y in held.get(b, []) if y[0] < e and a < y[1]]
                if not hit:
                    break
                t = max(y[1] for y in hit)
            if best is None or e < best[0]:
                best = (e, b, put)
        e, b, put = best
        for u, s in put:
            start[u] = s
            busy[ops[u]["q"]].append((s, s + ops[u]["c"]))
        held.setdefault(b, []).append((put[0][1], e, x))
        bank[x] = b
    for b in held:
        row = sorted(held[b])
        for y, z in zip(row, row[1:]):
            pre[users[z[2]][0]] |= set(users[y[2]])
    return sorted(range(n), key=lambda k: (start[k], k)), pre, bank


_LAID = {}


def rank_program(g, core, T, topo):
    rank = T.rank_of(core)
    if rank is None:
        return
    N = len(T.cores)
    qs = {"v": g.vector, "s": g.scalar, "p": g.tensor, "g": g, "y": g.sync}
    ops, wr, rd, bank, num = [], {}, {}, {}, {"P": 0, "W": 0, "C": 0, "U": 0}

    def ap(a):
        if isinstance(a, (int, float)):
            return a
        t = T[bank.get(a[0], a[0])]
        if len(a) == 5:
            return t[:, a[1]:a[2]].indirect(T[a[3]][:, a[4][0]:a[4][1]])
        return t[:, a[1]:a[2]:a[3]] if len(a) == 4 else t[:, a[1]:a[2]]

    def psum(a):
        return "#" in a[0]

    def note(q, reads, writes, fn, c, after=0.0, kind="c", shared=False):
        k, r, w_, tiles = len(ops), [], [], []
        for xs, to in ((reads, r), (writes, w_)):
            for a in xs:
                if isinstance(a, (int, float)):
                    continue
                if psum(a):
                    w_.append((a[0], 0, 512))
                    if a[0] not in tiles:
                        tiles.append(a[0])
                else:
                    to.append(a[:3])
                if len(a) == 5:
                    r.append((a[3], a[4][0], a[4][1]))
        pre = set()
        for n, lo, hi in r:
            pre |= {x[2] for x in wr.get(n, []) if x[0] < hi and lo < x[1]}
        for n, lo, hi in w_:
            pre |= {x[2] for x in wr.get(n, []) if x[0] < hi and lo < x[1] and not (shared and x[3])}
            pre |= {x[2] for x in rd.get(n, []) if x[0] < hi and lo < x[1]}
        for n, lo, hi in r:
            rd.setdefault(n, []).append((lo, hi, k))
        for n, lo, hi in w_:
            wr[n] = [x for x in wr.get(n, []) if shared or not (lo <= x[0] and x[1] <= hi)] + [(lo, hi, k, shared)]
            if not shared:
                rd[n] = [x for x in rd.get(n, []) if x[2] == k or not (lo <= x[0] and x[1] <= hi)]
        pre.discard(k)
        ops.append({"q": q, "pre": pre, "fn": fn, "c": c, "after": after, "kind": kind, "tiles": tiles})

    def size(a):
        return 16 * (a[4][1] - a[4][0]) if len(a) == 5 else (a[2] - a[1]) // (a[3] if len(a) == 4 else 1)

    def cost(o, a, k):
        n = size(o) * CFG["sc"] if len(o) == 5 else size(a) * CFG["ga"] if len(a) == 5 else max(64, size(o) * k)
        return CFG["fix"] + CFG["cyc"] * n

    def half(*xs):
        return 0.5 if all(not psum(a) and _SB[a[0]][1] in (B, U) for a in xs) else 1

    def dma(q, out, in_, reads, writes, kb, shared=False, **kw):
        note(q, reads, writes, lambda: qs[q].dma_start(out, in_, **kw), 0.1, CFG["dma"] + kb / 300, "d", shared)

    def tt(o, a, b, op):
        note("v", [a, b], [o], lambda: g.vector.tensor_tensor(ap(o), ap(a), ap(b), op), cost(o, a, 1 if psum(a) else 2))

    def ts(o, a, s1, op0, s2=None, op1=None):
        if s2 is None:
            note("v", [a, s1], [o], lambda: g.vector.tensor_scalar(ap(o), ap(a), ap(s1), None, op0), cost(o, a, half(o, a)))
        else:
            note("v", [a, s1, s2], [o], lambda: g.vector.tensor_scalar(ap(o), ap(a), ap(s1), ap(s2), op0, op1), cost(o, a, half(o, a)))

    def cp(o, a):
        note("v", [a], [o], lambda: g.vector.tensor_copy(ap(o), ap(a)), cost(o, a, half(o, a)))

    def ms(o, v):
        note("v", [], [o], lambda: g.vector.memset(ap(o), v), cost(o, o, half(o)))

    def act(o, a, f=AF.Identity, bias=0.0, scale=1.0, shared=False):
        bias, scale = [float(x) if isinstance(x, int) else x for x in (bias, scale)]
        note("s", [a, bias, scale], [o], lambda: g.scalar.activation(ap(o), ap(a), f, bias=ap(bias), scale=ap(scale)),
             cost(o, a, 1), shared=shared)

    def move(q, o, a):
        (act if q == "s" else cp)(o, a)

    def iota(o, pat, base=0, cm=0):
        kw = {} if _SB[o[0]][1] == I else {"allow_small_or_imprecise_dtypes": True}
        note("g", [], [o], lambda: g.iota(ap(o), pat, base, cm, **kw), 0.13 + 2 * CFG["cyc"] * size(o))

    def mm(ms_, start=True, stop=True):
        def fn():
            for k, (o, l, r) in enumerate(ms_):
                x = g.tensor.matmul(ap(o), ap(l), ap(r), start and k == 0, stop and k == len(ms_) - 1)
            return x
        c = sum(max(64, size(r)) * (4 if _SB[r[0]][1] == F else 1) for o, l, r in ms_)
        note("p", [x for o, l, r in ms_ for x in (l, r)], [ms_[0][0]], fn, CFG["pe"] * c)

    def tile(lo=0, hi=512):
        num["P"] += 1
        return ("P#%d" % num["P"], lo, hi)

    def tmp(c0=0, c1=64):
        num["W"] += 1
        k = num["W"] % NW
        return ("W", 64 * k + c0, 64 * k + c1)

    ID = {1: ("I1", 0, 128), -1: ("IN", 0, 128), 64: ("I64", 0, 128), 4096: ("I4K", 0, 128), -1536: ("I24", 0, 128)}
    IDF = {1: ("F1", 0, 128), -1: ("FN", 0, 128)}

    def lin(o, terms, f=AF.Identity, bias=0.0, scale=1.0):
        p = tile(0, o[2] - o[1])
        mm([(p, (IDF if _SB[x[0]][1] == F else ID)[c], x) for c, x in terms])
        act(o, p, f, bias, scale)

    def wrap(o, a, src, lo, hi):
        mm([(o, (a, 15 - i, 143 - i), (src, lo + i, hi, 16)) for i in range(16)])

    def spread(p, x, h):
        return [((p[0], i, 512, 16), ("SB", 128 * i, 128 * i + 128), (x[0], x[1] + 32 * h, x[1] + 32 * h + 32)) for i in range(16)]

    landed = {}

    def send(src, lo, dst, dlo, sem, sign):
        to = [T.cores[(rank + sign) % N], T.cores[(rank + 2 * sign) % N]]
        em = masks(topo, core, to[0], to[1])

        def fn():
            tr = []
            for h, d in enumerate(to):
                rid, pid, _ = topo.addr(d)
                tr.append(RemoteDMATransfer(dst_ids=[DstId(rid=rid, pnc=pid)], dma_engine_mask=sum(1 << e for e in em[h]),
                                            remote_sem=T.sem[sem], src=T[src][:, lo + 256 * h:lo + 256 * h + 256],
                                            dst=T[dst][:, dlo + 256 * h:dlo + 256 * h + 256]))
            g.remote_dma_fused(tr, local_sem=T.sem.ls)
            return len(em[0]) + len(em[1])
        note("g", [(src, lo, lo + 512)], [(sem, 0, 1)], fn, 0.5, 0.0, "r")
        n = 0
        for h in range(2):
            s = (rank - (h + 1) * sign) % N
            n += len(masks(topo, T.cores[s], T.cores[(s + sign) % N], T.cores[(s + 2 * sign) % N])[h])
        landed[sem] = n
        note("l", [(sem, 0, 1)], [(dst, dlo, dlo + 512)], sem, 0.01, CFG["rem"], "l")

    def w(n, t=0, c0=0, c1=64):
        return (n, 64 * t + c0, 64 * t + c1)

    def cut(x, c0):
        return (x[0], x[1] + c0, x[2])

    def col(k, n="COL"):
        return (n, k, k + 1)

    def slot(t, h):
        return ("G8", 512 * h, 512 * h + 512) if t == 8 else ("WX", SL + 1024 * t + 512 * h, SL + 1024 * t + 512 * h + 512)

    def fl(k, c0=0, c1=64):
        return w("FL", k, c0, c1)

    J, RT = ("E", 0, 64), ("E", 32, 96)

    dma("y", T.KI[:, 0:256], T.k0[:], [], [("KI", 0, 256)], 128)
    dma("s", T.KI[:, 256:512], T.k1[:], [], [("KI", 256, 512)], 128)
    dma("y", T.WX[:, 0:4096], T.x[:], [], [("WX", 0, 4096)], 1024)
    dma("s", T.Q[:, 512:1024], T.q[:], [], [("Q", 512, 1024)], 128)
    iota(("PI", 0, 1), [[0, 1]], 0, 1)
    iota(("N144", 0, 144), [[1, 144]])
    iota(("MG", 0, 128), [[16, 8], [0, 16]])
    iota(("E", 0, 256), [[16, 256]])
    ms(("TB", 0, 1024), 0.0)
    ms(("TB", 1024, 1536), 0.0)
    ms(("TB", 1536, 2560), 64.0)
    ms(("TB", 2560, 5120), 0.0)
    ts(("PI", 4, 5), ("PI", 0, 1), 15, AL.bitwise_and)
    cp(col(0), ("PI", 0, 1))
    cp(col(1), ("PI", 4, 5))
    ts(col(2), col(0), col(1), AL.subtract)
    ts(("M16", 0, 16), ("N144", 0, 16), col(1), AL.is_equal)
    ts(("A1", 0, 144), ("N144", 0, 144), -15.0, AL.add, col(2), AL.is_equal)
    ts(("I1", 0, 128), ("N144", 0, 128), col(0), AL.is_equal)
    ts(("BO", 0, 128), ("MG", 0, 128), col(2), AL.is_equal)
    for f in range(2):
        x = (256 * f, 256 * f + 256)
        for r, ki, kb, s, op in ((0, "KL", "DL", 63, AL.bitwise_and), (1, "KH", "DH", 6, AL.logical_shift_right)):
            ts((ki,) + x, ("KI",) + x, s, op)
            cp((kb,) + x, (ki,) + x)
            dma("ys"[r], T.TB[2 * f + r::16, 1024:5120], T[kb][:, x[0]:x[1]], [(kb,) + x], [("TB", 1024, 5120)], 64, True)

    def m16(r):
        return col(r, "M16")

    nc = 8
    for name, terms in (("AK0", ((0, 1), (1, 64), (4, -4096))), ("AK1", ((2, 1), (3, 64), (4, -4096))),
                        ("AX", ((5, 1), (6, 16), (7, 1024), (4, 64), (8, -81))),
                        ("AKW", ((6, 1), (5, 576), (7, 64), (8, -576), (9, -1)))):
        acc = m16(terms[0][0])
        for r, c in terms[1:]:
            act(col(nc), m16(r), bias=acc, scale=c)
            acc = col(nc)
            nc += 1
        act((name, 0, 144), ("A1", 0, 144), scale=acc)
    act(("A8", 0, 144), ("A1", 0, 144), scale=8192)
    for n, c in (("IN", -1), ("I64", 64), ("F1", 1), ("I4K", 4096), ("I24", -1536), ("FN", -1)):
        act((n, 0, 128), ("I1", 0, 128), scale=c)
    ts(("E", 0, 256), ("E", 0, 256), col(1), AL.add)
    act(("J8", 0, 64), J, bias=-8192)
    for i in range(16):
        ts(("SB", 128 * i, 128 * i + 128), ("BO", 0, 128), m16(i), AL.mult)
    ms(w("OK", 2), 0.0)
    ms(("DR", 0, 192), 0.0)
    ms(("WT", 0, 192), 0.0)
    ms(("H", 0, 192), 0.0)
    ms(("FL", 0, 384), 0.0)
    for n, v in (("AA", 0.0), ("GO", 1.0), ("DM", 0.0), ("RR", 0.0), ("ZP", 1.0)):
        ms((n, 0, 256), v)
    act(col(3), m16(4), scale=64)
    act(("BC", 0, 16), ("N144", 0, 16), bias=col(3), scale=m16(5))
    for i in range(16):
        act(("BASE", i, 1024, 16), ("N144", 0, 64), bias=col(i, "BC"), scale=m16(6), shared=True)
    for f in range(2):
        p = tile(0, 64)
        wrap(p, "AK%d" % f, "TB", 1536, 2560)
        ts(w("KR", f), p, 262144.0, AL.add)
        tt(w("KDR", f), w("KR", f), RT, AL.subtract)
        act(w("KDH", f), w("KDR", f), scale=0.5)
        tt(w("KDH", 2 + f), w("KDH", f), RT, AL.add)
    cp(w("c16", 0, 32), w("KR", 0, 32))
    act(w("C", 0, 32), w("KR", 0, 32))
    act(w("C", 3, 0, 32), w("KR", 1, 0, 32))
    cp(w("c16", 1, 0, 32), w("KR", 1, 0, 32))
    cp(("KF", 0, 512), ("KI", 0, 512))
    dma("g", T.yk0[:], T.KF[:, 0:256], [("KF", 0, 256)], [("yk0", 0, 1)], 128)
    dma("g", T.yk1[:], T.KF[:, 256:512], [("KF", 256, 512)], [("yk1", 0, 1)], 128)
    for k in range(12):
        iota(("WK", 768 * k, 768 * k + 768), [[0, 768]])
    for lo in (SL + 1024, SL + 2048, DUM, DUM + 512):
        iota(("WX", lo, lo + 512), [[0, 512]], -100)
    for f in range(2):
        iota(("KD%d" % f, 0, 576), [[0, 576]])
    ms(("TQ", 1024, 1040), 100.0)

    def first(t):
        return 32 if t < 3 else 0

    def halves(t):
        return [1] if t < 3 else [1, 0]

    def ask(t):
        c0, hs, f = first(t), halves(t), t & 1
        o = slot(t, 0)
        act((o[0], o[1] + 16 * c0, o[1] + 1024), ("WX", 0, 4096, "c16", (64 * f + c0, 64 * f + 64)))
        for h in range(2):
            a, b = c0 + (64 - c0) // 2 * h, c0 + (64 - c0) // 2 * (h + 1)
            move(CFG["kg"][h], ("KG", 16 * a, 16 * b), ("TB", 1024, 5120, "c16", (64 * f + a, 64 * f + b)))
        act(w("C8", t, c0), w("C", t, c0), bias=-7168)
        dep = [(1, w("DM", t, c0)), (1, w("RR", t, c0))]
        if t == 8:
            lin(w("ZZ"), dep, AF.Relu, 1, -1)
        else:
            act(w("SG", t, c0), w("C", t, c0), AF.Sign, 511.5, -1)
            extra = [(-1, w("DR", k)) for k in range(3)] if t == 5 else []
            go = [(-1, w("GO", t - 1, c0)), (1, w("DR", t - 1, c0))] if t % 3 else [(-1, w("GO", t, c0))]
            p = tile(c0, 64)
            mm([(p, ID[c], x) for c, x in dep + go + extra])
            act(w("ZP", t + 1, c0), p, AF.Sign, 0.5, -1)
            act(w("DM", t + 1, c0), p, AF.Relu)
            x = tmp(c0)
            tt(x, w("ZP", t + 1, c0), w("KDH", 1 - f, c0), AL.mult)
            tt(w("ALT", t, c0), x, w("KDH", 3 - f, c0), AL.add)
            if t == 5:
                x = tmp(32)
                tt(x, fl(0, 32), w("KAD", 0, 32), AL.mult)
                tt(w("ALT", t, 32), w("ALT", t, 32), x, AL.add)
            iota(("TT", 1024 * f + 16 * c0, 1024 * f + 1024), [[0, 1024 - 16 * c0]], t)
        for h in hs:
            pa = tile()
            mm([(pa, ID[1], slot(t, h))] + spread(pa, w("AA", t), h), stop=False)
            mm([(pa, ID[-1], x) for x in qt[h]], start=False)
            if CFG["cmp"][1 - h] == "v":
                ts(("CMP", 512 * h, 512 * h + 512), pa, 0.0, AL.is_ge, 0.5, AL.subtract)
            else:
                act(("CMP", 512 * h, 512 * h + 512), pa, AF.Sign, 0.5)
        pk = tile(c0, 64)
        wrap(pk, "AK%d" % (1 - f), "KG", 16 * c0, 1024)
        if t == 0:
            p = tile(32, 64)
            wrap(p, "AK0", "KG", 512, 1024)
            tt(w("KAD", 0, 32), p, cut(RT, 32), AL.subtract)
        return pk[0]

    def raise_(o, terms, up, spr, q):
        p = tile()
        if q == "v":
            mm([(p, ID[1], up)] + spr(p))
            tt(o, p, o, AL.max)
            return [o]
        num["U"] += 1
        u = ("UQ", 512 * (num["U"] & 1), 512 * (num["U"] & 1) + 512)
        mm([(p, ID[1], up)] + [(p, ID[-1], x) for x in terms] + spr(p))
        act(u, p, AF.Relu)
        p = tile()
        mm([(p, ID[1], x) for x in terms + [u]])
        act(o, p)
        return [o]

    def signs():
        num["C"] += 1
        return 1024 * (num["C"] % 3)

    def pair(parent, child, mask_, hs, flag):
        lo = signs()
        for h in hs:
            p = tile()
            mm([(p, ID[1], slot(child, h)), (p, ID[-1], slot(parent, h))])
            act(("CM2", lo + 512 * h, lo + 512 * h + 512), p, AF.Sign, 0.5)
            raise_(slot(parent, h), [slot(parent, h)], slot(child, h), lambda p: spread(p, mask_, h), CFG["ps"][parent + 1 if flag[1] else 0])
        c0 = 32 * min(hs)
        p = tile(c0, 64)
        wrap(p, "A1", "CM2", lo + 16 * c0, lo + 1024)
        tt(cut(flag, c0), p, cut(mask_, c0), AL.is_lt)

    def gate(k, part, t):
        o, m = ("GV", 512 * k, 512 * k + 512), w("M", 8 + 2 * k + part, 0, 32)
        if part == 0:
            act(m, w("H", t, 0, 32), bias=-129, scale=128)
        else:
            x = fl(32 + k, 0, 32)
            lin(x, [(1, w("OK", t, 0, 32)), (-1, w("OK", t - 1, 0, 32)), (-1, w("DR", t, 0, 32)), (-1, w("OK", t + 1, 0, 32))], AF.Relu)
            act(m, x, bias=-129, scale=128)
        p = tile()
        mm([(p, ID[1], slot(t, 0))] + spread(p, m, 0))
        tt(o, p, o if part else ("WX", 512, 1024), AL.max)

    def mask(k, terms, c0):
        lin(w("M", k, c0), [(1, cut(x, c0)) for x in terms], bias=-129, scale=128)

    def diffs(tau):
        c0 = first(tau - 1)
        lin(w("E1", tau, c0), [(1, w("C", tau - 1, c0)), (-1, w("C", tau, c0))])
        c2 = 64 if tau == 1 else first(tau - 2)
        if c2 > c0:
            lin(w("E2", tau, c0, c2), [(1, ("E", 32 + c0, 32 + c2)), (-1, w("C", tau, c0, c2))])
        if c2 < 64:
            lin(w("E2", tau, c2), [(1, w("XS", tau - 2, c2)), (-1536, w("OK", tau - 2, c2)), (-1, w("C", tau, c2))], bias=8704)
            if tau == 7:
                y = tmp(32)
                tt(y, fl(1, 32), w("CR", 0, 32), AL.mult)
                tt(w("E2", 7, 32), w("E2", 7, 32), y, AL.add)

    def link(tau, gterms, last):
        c0 = first(tau - 1)
        o = w("KD%d" % (tau & 1), tau - 1, c0)
        e1, e2 = w("E1", tau, c0), w("E2", tau, c0)
        beta = [(1, w("OK", tau, c0))] + [(-1, cut(x, c0)) for x in gterms]
        if last:
            ts(fl(21 + tau, c0), fl(12, c0) if tau == 7 else w("SG", 1, c0), float(8 - tau), AL.is_equal)
            beta.append((-1, fl(21 + tau, c0)))
            tt(w("Y", tau, c0), fl(21 + tau, c0), e1, AL.mult)
        lin(fl(34 + tau, c0), beta)
        terms = [(1, w("Y", tau, c0))] if last else []
        if gterms:
            tt(w("C8", tau, c0), w("AF", tau, c0), e1, AL.mult)
            terms.append((1, w("C8", tau, c0)))
        tt(e2 if terms else o, fl(34 + tau, c0), e2, AL.mult)
        if terms:
            lin(o, [(1, e2)] + terms)

    G = {1: [w("H", 1), w("H", 2), fl(3)], 2: [w("H", 2), w("H", 3), fl(2)], 3: [w("H", 3), w("H", 4)],
         4: [w("H", 4), w("H", 5)], 5: [w("H", 5)], 6: [w("H", 6)], 7: [], 8: []}
    qt = [[("Q", 0, 512)], [("Q", 512, 1024)]]
    for t in range(9):
        pk = ask(t)
        c0, hs, f = first(t), halves(t), t & 1
        ok = w("OK", t, c0)
        for a, b in ((32, 64), (0, 32)) if t in CFG["split"] else ((c0, 64),):
            pc = tile(a, b)
            wrap(pc, "A8", "CMP", 16 * a, 16 * b)
            m, o, x = tmp(a, b), w("OK", t, a, b), tmp(a, b)
            tt(x, pc, w("C8", t, a, b), AL.min)
            tt(m, (pk, a, b), x, AL.min)
            ts(o, m, -7168.0, AL.is_ge)
            if t == 8:
                continue
            x = tmp(a, b)
            tt(x, (pk, a, b), w("ALT", t, a, b), AL.subtract)
            tt(x, x, o, AL.mult)
            tt(w("C", t + 1, a, b), x, w("ALT", t, a, b), AL.add)
            cp(w("c16", 1 - f, a, b), w("C", t + 1, a, b))
            tt(w("XS", t, a, b), m, w("J8", 0, a, b), AL.max)
            ts(w("s16", f, a, b), w("XS", t, a, b), 8192.0, AL.add)
            lin(w("AN", t, a, b), [(1, w("AA", t, a, b)), (64, o)], bias=-64)
        if t in (0, 6):
            lin(w("CR", t, 32), [(1, w("C", t, 32)), (-1, cut(RT, 32))])
        if t > 0:
            diffs(t)
        if t == 8:
            break
        for h in hs:
            lo = 512 * h
            tt(("TB", 0, 5120, "s16", (64 * f + 32 * h, 64 * f + 32 * h + 32)), ("BASE", lo, lo + 512),
               ("TT", 1024 * f + lo, 1024 * f + lo + 512), AL.add)
            ops[-1]["pri"] = CFG["mp"][h]
            qt[h] = raise_(("Q", lo, lo + 512), qt[h], slot(t, h), lambda p: spread(p, w("AN", t), h),
                           "s" if len(qt[h]) > 1 else CFG["qs"][h] if t > 2 else "v")
        s1 = [(1, w("DR", k)) for k in range(3)] if t == 5 else []
        lin(w("AA", t + 1, c0), [(1, w("AA", t, c0)), (1, ok), (1, w("GO", t, c0))] + s1)
        lin(w("DR", t, c0), [(64, ok), (1, w("SG", t, c0))], AF.Relu, -31.5, 0.5)
        lin(w("GO", t + 1, c0), [(1, w("GO", t, c0)), (-1, w("DR", t, c0))] + s1)
        lin(w("RR", t + 1, c0), [(1, w("DM", t, c0)), (1, w("RR", t, c0)), (-1, w("DM", t + 1, c0)), (64, ok)], AF.Relu, -63)
        lin(w("WT", t, c0), [(1, ok), (1, ok), (1, w("ZP", t, c0))] + ([(-1, w("OK", t - 1, c0))] * 2 if t else []),
            AF.Relu, t / 2 - 4, 4 - t / 2)
        if t < 6:
            tt(w("DC", t, c0), w("DR", t, c0), w("C", t, c0), AL.mult)
        if t > 1:
            u, cu = t - 1, first(t - 1)
            lin(w("H", u, cu), [(1, w("OK", u, cu)), (-1, w("OK", t, cu))] + ([(-1, w("DR", u, cu))] if u > 2 else []), AF.Relu)
        if t in (2, 5):
            k = t // 3
            act(w("M", 12 + k, c0), w("AA", t + 1, c0), bias=-97 * k, scale=-1)
            for h in hs:
                p = tile()
                mm([(p, ID[1], ("Q", 512 * h, 512 * h + 512))] + spread(p, w("M", 12 + k), h))
                act(("TQ", 512 * h, 512 * h + 512), p)
            p, n, x, y = tile(0, 32), 512 << k, tmp(0, 32), tmp(0, 32)
            wrap(p, "AX", "TB", 1024, 1536)
            cp(("WI", 0, 32), p)
            ts(x, p, 4096.0 + 3072 * k, AL.is_lt, float(n), AL.mult)
            ts(("WI", 32, 64), ("WI", 0, 32), n - 1, AL.bitwise_and)
            tt(y, ("WI", 32, 64), x, AL.max)
            cp(w("o16", 0, 32 * k, 32 * k + 32), y)
            cp(("QG", 512 * k, 512 * k + 512), ("TQ", 1024 - n, 1040, "o16", (32 * k, 32 * k + 32)))
            send("QG", 512 * k, ("Q", "RQ")[k], 0, "e%d" % k, 1)
            if k:
                qt[0].append(("RQ", 0, 512))
            else:
                ms(("TQ", 1024, 1040), 0.0)
            lo = (SL, RV2)[k]
            act(y, x, bias=lo, scale=-lo / n)
            tt(("DO", 0, 32), y, ("DO", 0, 32) if k else ("E", 0, 32), AL.add)
            lin(w("DC", 6 + k, c0), [(1, w("DC", 3 * k + j, c0)) for j in range(3)])
        if t == 1:
            lin(fl(0, 32), [(1, w("DR", 1, 32)), (1, w("OK", 0, 32))], AF.Relu, -1)
        if t == 2:
            d, x = [w("DR", k, 32) for k in range(3)], tmp(32)
            lin(x, [(-1, d[0]), (-1, d[0]), (-1, d[0]), (-1, d[1]), (1, d[2])], bias=1536, scale=512)
            tt(x, x, ("E", 32, 64), AL.add)
            cp(w("o16", 1, 32), x)
            cp(w("o16", 1, 0, 32), w("DC", 6, 32))
        if t in (4, 7):
            gate(t // 7, 0, t - 1)
        if t == 5:
            gate(0, 1, 4)
            send("GV", 0, "WX", SL, "v1", -1)
            lin(fl(2), [(1, w("OK", 3)), (1, w("H", 4))], AF.Relu, -1)
            lin(fl(3), [(1, w("OK", 2)), (1, w("H", 3))], AF.Relu, -1)
            lin(fl(4), [(1, w("DR", k)) for k in (3, 4, 5)])
            x = tmp()
            act(x, fl(4), scale=RV2)
            lin(w("DC", 7), [(1, w("DC", 7)), (1, x)])
            act(("T3", 0, 512), ("WX", SL, SL + 512, "o16", (64, 96)))
            cp(("WX", SL, SL + 3072, "o16", (96, 128)), ("T3", 0, 512))
        if t == 6:
            lin(fl(1, 32), [(1, fl(0, 32)), (1, w("OK", 6, 32))], AF.Relu, -1)
            for k in (5, 4, 3, 2, 1):
                mask(k, G[k], first(k - 1))
                pair(k - 1, k, w("M", k), halves(k - 1), w("AF", k))
        if t == 7:
            mask(6, G[6], 0)
            pair(5, 6, w("M", 6), [1, 0], w("AF", 6))
            lin(fl(5, 32), [(1, fl(0, 32)), (1, w("H", 6, 32))], AF.Relu, -1)
            mask(7, [fl(5)], 32)
            pair(0, 6, w("M", 7), [1], w("AF", 0))

    gate(1, 1, 7)
    send("GV", 512, "WX", RV2, "v2", -1)
    px, pw = tile(0, 160), tile(0, 160)
    wrap(px, "AX", "TB", 2560, 5120)
    wrap(pw, "AKW", "TB", 2560, 5120)
    lin(fl(6), [(1, w("WT", k)) for k in (0, 2, 4, 6)])
    lin(fl(7), [(1, w("WT", k)) for k in (1, 3, 5, 7)])
    lin(fl(8), [(1, fl(6)), (-1, fl(7))], AF.Relu)
    lin(fl(9), [(1, fl(6)), (-1, fl(8))])
    ts(fl(10), fl(9), 1.0, AL.min)
    z7, dep = w("ZZ"), [w("DM", 8), w("RR", 8)]
    lin(fl(15), [(1, z7), (1, fl(10))], AF.Relu, 1, -1)
    lin(fl(16), [(-1, fl(7)), (-1, fl(8)), (64, fl(15))], AF.Relu, 0, -1)
    lin(fl(17), [(1, fl(9)), (64, z7)], AF.Relu, -64)
    x, lo = tmp(), signs()
    act(x, fl(16), bias=DUM - SL, scale=-1024)
    tt(x, x, J, AL.add)
    cp(w("o16", 2), x)
    for h in range(2):
        c, r = ("T1", 512 * h, 512 * h + 512), ("WX", 512 + 512 * h, 1024 + 512 * h)
        x = ("WX", SL, RV2, "o16", (128 + 32 * h, 160 + 32 * h))
        if CFG["rg"][h] == "s":
            act(c, x, bias=-1)
        else:
            ts(c, x, -1.0, AL.add)
        p = tile()
        mm([(p, ID[1], c), (p, ID[-1], r)])
        act(("CM2", lo + 512 * h, lo + 512 * h + 512), p, AF.Sign, 1.5)
        p = tile()
        mm([(p, ID[1], c)])
        tt(r, p, r, AL.max)
    p = tile(0, 64)
    wrap(p, "A1", "CM2", lo, lo + 1024)
    ts(fl(13), p, 0.0, AL.is_ge)
    lin(w("SG", 0), [(1, w("GO", 8)), (1, fl(4)), (-1, z7)], AF.Relu)
    lin(fl(11), [(1, w("SG", 0)), (-1, w("OK", 8))], AF.Relu)
    lin(fl(18), [(1, fl(7)), (1, fl(8)), (-1, fl(9)), (64, fl(10))], AF.Relu, -64)
    lin(fl(19), [(1, fl(1)), (1, w("OK", 7))], AF.Relu, -1)
    lin(fl(20), [(1, fl(7)), (1, fl(8)), (-1, fl(18)), (-1, dep[0]), (-1, dep[1])] + [(-1, fl(19))] * 5)
    lin(w("SG", 1), [(1, fl(20)), (64, w("SG", 0))], AF.Relu, -63)
    lin(w("SG", 2), [(1, w("SG", 1)), (1, fl(17))])
    lin(fl(12), [(1, w("SG", 2)), (-1, w("OK", 8))], AF.Relu)
    lin(fl(30), [(1, dep[0]), (1, dep[1])], AF.Sign, -1.5)
    lin(fl(31), [(64, fl(11)), (1, fl(30))], AF.Relu, -32, 0.5)
    x, y = tmp(), tmp()
    lin(x, [(-1, fl(12)), (64, fl(31)), (64, fl(31))], AF.Relu, -53.5 * 1024, 1024)
    tt(x, x, RT, AL.add)
    cp(w("o16", 4), x)
    act(y, fl(12), bias=DUM, scale=-1024)
    tt(y, y, J, AL.add)
    tt(y, y, w("DC", 7), AL.max)
    cp(w("o16", 5), y)
    act(("MX", 0, 32), ("DO", 0, 32))
    act(("MX", 32, 96), RT)
    tt(("MX", 96, 256), px, ("E", 96, 256), AL.max)
    cp(("x16", 0, 256), ("MX", 0, 256))
    ms(("MK", 0, 32), 0.0)
    act(col(4), col(1), bias=512, scale=576)
    act(("MK", 32, 96), ("N144", 0, 64), bias=col(4))
    cp(("k16", 0, 96), ("MK", 0, 96))
    cp(("k16", 96, 256), pw)
    lo = signs()
    for h in range(2):
        a, b, c = [(n, o + 512 * h, o + 512 * h + 512) for n, o in (("T1", 1024), ("T2", 0), ("T3", 0))]
        move(CFG["lp"][h], b, ("WX", 0, DUM, "o16", (256 + 32 * h, 288 + 32 * h)))
        move(CFG["lc"][h], a, ("WX", 0, 13824, "o16", (320 + 32 * h, 352 + 32 * h)))
        p = tile()
        mm([(p, ID[1], a), (p, ID[-1], b)])
        if CFG["uq"][h] == "v":
            ts(c, p, -1.0, AL.add, 0.0, AL.max)
        else:
            act(c, p, AF.Relu, -1)
        act(("CM2", lo + 512 * h, lo + 512 * h + 512), p, AF.Sign, 0.5)
    tt(("WX", 0, DUM, "o16", (256, 320)), ("T2", 0, 1024), ("T3", 0, 1024), AL.add)
    ops[-1]["pri"] = CFG["pri"]
    p = tile(0, 64)
    wrap(p, "A1", "CM2", lo, lo + 1024)
    ts(fl(21), p, 0.0, AL.is_ge)
    for tau in range(1, 9):
        link(tau, G[tau], tau in (1, 3, 4, 5, 7))
    x, y = tmp(32), tmp(32)
    lin(fl(43, 32), [(1, fl(1, 32)), (-1, fl(5, 32))], scale=-1)
    tt(x, w("CR", 0, 32), w("CR", 6, 32), AL.subtract)
    tt(x, x, w("AF", 0, 32), AL.mult)
    tt(y, fl(43, 32), w("CR", 6, 32), AL.mult)
    tt(w("KD0", 0, 32), x, y, AL.add)
    ea, pa = fl(13), fl(44)
    tt(pa, fl(7), fl(6), AL.is_gt)
    lin(fl(45), [(1, ea), (1, pa)], AF.Relu, -1)
    lin(fl(47), [(1, w("OK", 8)), (1, z7)], AF.Relu, -1)
    ts(w("AF", 7), fl(6), 1.0, AL.min)
    ts(w("AF", 8), fl(7), 1.0, AL.min)
    lin(w("H", 7), [(1, ea), (-1, fl(45)), (-1, w("AF", 7)), (-1, fl(47))])
    lin(w("H", 8), [(1, fl(45)), (-1, w("AF", 8))])

    def late(o, y, e, sign):
        if CFG["tail"] == "v":
            tt(y, y, e, AL.mult)
            tt(o, o, y, AL.add if sign > 0 else AL.subtract)
        else:
            lin(y, [(-sign, y), (4096, e), (4096, e)], AF.Relu, -4096)
            lin(o, [(1, o), (-1, y), (4096, e)])

    for f, taus in ((0, (4,)), (1, (1, 3, 5, 7))):
        n, y = "KD%d" % f, w("Y", 2 * f)
        tt(w(n, 8), w("H", 7 + f), w("KDR", f), AL.mult)
        tt(w("AN", f), w("SG", 2), fl(6 + f), AL.is_equal)
        tt(y, w("AN", f), w("KDR", f), AL.mult)
        for tau in taus:
            c0 = first(tau - 1)
            late(w(n, tau - 1, c0), w("Y", tau, c0), fl(21, c0), -1)
        late(w(n, 8), y, fl(21), 1)
        dma("y", T.WK[f::16, :], T[n][:], [(n, 0, 576)], [("WK", 0, 9216)], 288, True)
    for k in range(4):
        o = ("XO", 1024 * k, 1024 * k + 1024)
        move(CFG["xq"][k], o, ("WX", 0, 13824, "x16", (64 * k, 64 * k + 64)))
        dma("y", T.yx[:, o[1]:o[2]], ap(o), [o], [], 256)
        move(CFG["kq"][k], ("YK", o[1], o[2]), ("WK", 0, 9216, "k16", (64 * k, 64 * k + 64)))
    for f in range(2):
        dma("g", T["yk%d" % f][:], T.YK[f::16, :], [("YK", 0, 4096), ("yk%d" % f, 0, 1)], [], 256, accum_op=AL.add, max_dma_last_dim=8192)

    if "x" not in _LAID:
        _LAID["x"] = layout(ops)
    seq, pre, banks = _LAID["x"]
    bank.update(banks)
    cnt, seen, tok, nd = {"sv": 0, "ss": 0, "sp": 0, "sg": 0, "ls": 0}, {q: {} for q in qs}, {}, 0

    def wait(q, s, n):
        if seen[q].get(s, 0) < n and not (q == "p" and s == "sp"):
            qs[q].wait_ge(T.sem[s], n)
            seen[q][s] = n

    for k in seq:
        o = ops[k]
        if o["kind"] == "l":
            tok[k] = (o["fn"], landed[o["fn"]])
            cnt[o["fn"]] = landed[o["fn"]]
            continue
        need = {}
        for p in pre[k]:
            need[tok[p][0]] = max(need.get(tok[p][0], 0), tok[p][1])
        for s in need:
            wait(o["q"], s, need[s])
        if o["kind"] == "r":
            cnt["ls"] += o["fn"]()
            continue
        s, n = ("s" + o["q"], 1) if o["kind"] == "c" else ("d%d" % nd, 16)
        nd += o["kind"] == "d"
        cnt[s] = cnt.get(s, 0) + n
        o["fn"]().then_inc(T.sem[s], n)
        tok[k] = (s, cnt[s])
    for s in cnt:
        wait("g", s, cnt[s])
